import numpy as np
import ml_dtypes


def mxq(x, axis, fmt="e4m3"):
    dtype, down = {"e4m3": (ml_dtypes.float8_e4m3fn, 7), "e5m2": (ml_dtypes.float8_e5m2, 14)}[fmt]
    v = np.moveaxis(np.asarray(x, np.float32).astype(ml_dtypes.bfloat16).astype(np.float64), axis, -1)
    blocks = v.reshape(v.shape[:-1] + (-1, 32))
    amax = np.abs(blocks).max(-1, keepdims=True)
    byte = np.maximum(np.where(amax > 0, np.frexp(amax)[1] - 1 + 127, 0) - down, 1)
    scale = np.exp2(byte - 127.0)
    codes = (blocks / scale).astype(np.float32).astype(dtype).astype(np.float64)
    return np.moveaxis((codes * scale).reshape(v.shape), -1, axis)


WIDE = False


def mx_kscale(k, group=512):
    if not WIDE:
        return np.ones(k)
    levels = np.array([10, -10, 5, -5, 0])
    if group != 512:
        return np.exp2(np.random.permutation(np.resize(levels, k // group))).repeat(group)
    if k % 512:
        return np.exp2(np.random.permutation(np.resize(levels, k // 32))).repeat(32)
    a = np.empty((k // 512, 16))
    for p in range(k // 512):
        a[p, :8] = np.random.permutation(np.resize(levels, 8))
        for g in range(8):
            far = levels[np.abs(levels - a[p, g]) >= 10]
            a[p, g + 8] = far[np.random.randint(len(far))]
    return np.exp2(a.ravel()).repeat(32)


def f64(x):
    return np.asarray(x).astype(np.float64)


E2M1 = np.array([0.0, 0.5, 1.0, 1.5, 2.0, 3.0, 4.0, 6.0, -0.0, -0.5, -1.0, -1.5, -2.0, -3.0, -4.0, -6.0])


def pack_group(w):
    k, n = w.shape
    w = f64(np.asarray(w, np.float32).astype(ml_dtypes.bfloat16)).reshape(k // 32, 32, n)
    amax = np.abs(w).max(1)
    mant, ex = np.frexp(amax / 6.0)
    byte = np.clip(np.where(amax > 0, np.where(mant > 0.5, ex, ex - 1) + 127, 1), 1, 254)
    scaled = (w * np.exp2(127.0 - byte)[:, None, :]).reshape(k, n).astype(np.float32)
    c = np.ascontiguousarray(scaled.reshape(k // 4, 4, n).transpose(0, 2, 1)).astype(ml_dtypes.float4_e2m1fn).view(np.uint8) & 0xF
    return np.ascontiguousarray((c[..., 0::2] | (c[..., 1::2] << 4)).reshape(k // 4, 2 * n)), byte.astype(np.uint8)


def unpack_group(words, scales):
    p, n = words.shape[0], scales.shape[1]
    words = np.ascontiguousarray(words).reshape(p, n, 2)
    nib = np.empty((p, n, 4), np.uint8)
    nib[..., 0::2] = words & 0xF
    nib[..., 1::2] = words >> 4
    return E2M1[nib].transpose(0, 2, 1).reshape(4 * p, n) * np.repeat(np.exp2(scales.astype(np.float64) - 127.0), 32, axis=0)


def silu(v):
    return v / (1.0 + np.exp(-v))


G, D, M, N = 4, 256, 128, 1024


def setup_inputs():
    n = np.random.standard_normal
    s = mx_kscale(D, 0)[:, None]
    w_ = [pack_group(w) for w in n((G, D, M)) / np.sqrt(D) / s]
    u_ = [pack_group(w) for w in n((G, D, M)) / np.sqrt(D) / s]
    return {
        "x": (n((G, D, N)) * s).astype(np.float32),
        "w_words": np.stack([w[0] for w in w_]),
        "w_scales": np.stack([w[1] for w in w_]),
        "u_words": np.stack([w[0] for w in u_]),
        "u_scales": np.stack([w[1] for w in u_]),
        "b": (0.5 * n((G, M, 1))).astype(np.float32),
    }


def reference(x, w_words, w_scales, u_words, u_scales, b):
    xq = mxq(f64(x), 1, "e4m3")
    h = np.stack([unpack_group(w_words[g], w_scales[g]) for g in range(G)]).transpose(0, 2, 1) @ xq
    g = np.stack([unpack_group(u_words[g], u_scales[g]) for g in range(G)]).transpose(0, 2, 1) @ xq
    h = h + f64(b)
    y = silu(h) * g
    return y

@@ -1,0 +1,163 @@
+from contextlib import ExitStack
+
+import concourse.mybir as mybir
+
+G, D, M, N = 4, 256, 128, 1024
+FLOPS = 2 * 2 * G * D * M * N
+
+F32 = mybir.dt.float32
+BF16 = mybir.dt.bfloat16
+I32 = mybir.dt.int32
+U32 = mybir.dt.uint32
+U8 = mybir.dt.uint8
+FP8X4 = mybir.dt.float8_e4m3fn_x4
+FP4X4 = mybir.dt.float4_e2m1fn_x4
+SILU = mybir.ActivationFunctionType.Silu
+MULT = mybir.AluOpType.mult
+ADD = mybir.AluOpType.add
+
+P = 128
+ROWS = 64
+UNIT = 256
+WIN = 512
+UNITS = 8
+V_COLS = [256,160,144,144,144,144,144,160]
+G_COLS = [0,0,0,0,0,0,0,0]
+LOADS = [[0,1],[1,1],[2,1],[3,1],[4,2],[6,1],[7,1]]
+
+
+def tile_rows_gglu_silu_bias_kernel(tc, x, w_words, w_scales, u_words, u_scales, b, out):
+    nc = tc.nc
+    with ExitStack() as ctx:
+        keep = ctx.enter_context(tc.tile_pool(name="keep", bufs=1))
+        psum = ctx.enter_context(tc.psum_pool(name="psum", bufs=1))
+        ctx.enter_context(tc.manual_schedule())
+
+        x_pairs = x.rearrange("(q c) (p j) n -> q (c p) j n", c=2, j=4)
+        words = [keep.tile([P, 2, 2 * M], U8, name="words%d" % t, align_bytes=64) for t in range(2)]
+        planes = [keep.tile([P, 2, M], U8, name="planes%d" % t, align_bytes=64) for t in range(2)]
+        bias_rows = keep.tile([P, P], F32, name="bias_rows", align_bytes=64)
+        bias_cols = keep.tile([P, P], F32, name="bias_cols", align_bytes=64)
+        warm_in = keep.tile([P, 8], F32, name="warm_in")
+        warm_out = keep.tile([P, 8], F32, name="warm_out")
+        codes = keep.tile([P, UNIT * (UNITS + 1)], U32, name="codes", align_bytes=64)
+        scales = keep.tile([P, UNIT * (UNITS + 1)], U8, name="scales", align_bytes=64)
+        raw = [keep.tile([P, 4, UNIT], F32, name="raw%d" % u, align_bytes=64) for u in range(2)]
+        raw_rest = keep.tile([P, 4, 4 * UNIT], F32, name="raw_rest", align_bytes=64)
+        grouped = [keep.tile([P, UNIT, 4], BF16, name="grouped%d" % u, align_bytes=64) for u in range(8)]
+        act = [keep.tile([P, 2, UNIT], F32, name="act%d" % u, align_bytes=64) for u in range(UNITS)]
+        y = [keep.tile([P, 2, N], F32, name="y%d" % q, align_bytes=64) for q in range(2)]
+        acc = [[[psum.tile([P, WIN], F32, name="acc%d%d%d" % (s, t, c)) for c in range(2)] for t in range(2)] for s in range(2)]
+
+        def raw_of(u0, count):
+            if u0 < 2 or u0 >= 6:
+                return raw[u0 % 2][:, :, :]
+            return raw_rest[:, :, (u0 - 2) * UNIT : (u0 - 2 + count) * UNIT]
+
+        def load_x(i):
+            u0, count = LOADS[i]
+            n0 = (u0 % 4) * UNIT
+            nc.sync.dma_start(out=raw_of(u0, count), in_=x_pairs[u0 // 4][:, :, n0 : n0 + count * UNIT])
+
+        def load_words(eng, t):
+            src = (w_words, u_words)[t].bitcast(I32).rearrange("(q c) p n -> (c p) q n", c=2)
+            eng.dma_start(out=words[t][:].bitcast(I32), in_=src)
+
+        def load_plane(eng, t, quad):
+            src = (w_scales, u_scales)[t].bitcast(I32).rearrange("(q c) (h r) m -> c h r q m", c=2, h=2)
+            eng.dma_start(out=planes[t][32 * quad : 32 * quad + 4].bitcast(I32), in_=src[quad // 2, quad % 2])
+
+        def interleave(u, lo, hi):
+            src = raw_of(u, 1)[:, :, lo:hi].rearrange("p t (c i) -> p c t i", i=4)
+            dst = grouped[u % 8][:, lo:hi, :].rearrange("p (c i) t -> p c t i", i=4)
+            return src, dst
+
+        def copy_v(u):
+            if V_COLS[u] > 0:
+                src, dst = interleave(u, 0, V_COLS[u])
+                nc.vector.tensor_copy(out=dst, in_=src)
+
+        def copy_g(u):
+            if G_COLS[u] > 0:
+                src, dst = interleave(u, V_COLS[u], V_COLS[u] + G_COLS[u])
+                nc.gpsimd.tensor_scalar(out=dst, in0=src, scalar1=1.0, scalar2=0.0, op0=MULT, op1=ADD)
+
+        def copy_s(u):
+            if V_COLS[u] + G_COLS[u] < UNIT:
+                src, dst = interleave(u, V_COLS[u] + G_COLS[u], UNIT)
+                nc.scalar.copy(out=dst, in_=src)
+
+        def quantize(u):
+            cols = slice((u + 1) * UNIT, (u + 2) * UNIT)
+            nc.vector.quantize_mx(out=codes[:, cols].bitcast(FP8X4), scales=scales[:, cols], in_=grouped[u % 8][:].rearrange("p n t -> p (n t)"))
+
+        def multiply(u):
+            win = slice(u * UNIT, u * UNIT + WIN)
+            for t in range(2):
+                for c in range(2):
+                    rows = slice(ROWS * c, ROWS * (c + 1))
+                    nc.tensor.matmul_mx(
+                        out=acc[u % 2][t][c][:],
+                        lhsT=words[t][rows, u // 4, :].bitcast(FP4X4),
+                        lhsT_scale=planes[t][rows, u // 4, :],
+                        rhs=codes[rows, win].bitcast(FP8X4),
+                        rhs_scale=scales[rows, win],
+                        start=True,
+                        stop=True,
+                    )
+
+        def silu(u, c):
+            g = 2 * (u // 4) + c
+            nc.scalar.activation(out=act[u][:, c, :], in_=acc[u % 2][0][c][:, UNIT:WIN], func=SILU, bias=bias_cols[:, 32 * g : 32 * g + 1])
+
+        def gate(u, c):
+            n0 = (u % 4) * UNIT
+            nc.vector.tensor_tensor(out=y[u // 4][:, c, n0 : n0 + UNIT], in0=acc[u % 2][1][c][:, UNIT:WIN], in1=act[u][:, c, :], op=MULT)
+            q = u // 4
+            if u == UNITS - 1:
+                nc.sync.dma_start(out=out[2 * q + c, :, n0 : n0 + UNIT], in_=y[q][:, c, n0 : n0 + UNIT])
+            elif c == 1 and (u % 2 == 1 or u == UNITS - 2):
+                lo = n0 if u == UNITS - 2 else n0 - UNIT
+                nc.sync.dma_start(out=out[2 * q : 2 * q + 2, :, lo : n0 + UNIT].rearrange("c m n -> m c n"), in_=y[q][:, :, lo : n0 + UNIT])
+
+        nc.vector.memset(planes[0][:].rearrange("p q m -> p (q m)").bitcast(I32), 0)
+        nc.gpsimd.memset(bias_rows[:], 0.0)
+        nc.vector.memset(warm_in[:], 0.0)
+        nc.vector.memset(planes[1][:].rearrange("p q m -> p (q m)").bitcast(I32), 0)
+        nc.vector.memset(codes[:, 0:UNIT], 0)
+        nc.vector.memset(scales[:, 0:UNIT].bitcast(I32), 0)
+        load_x(0)
+        load_words(nc.sync, 0)
+        for quad in range(4):
+            load_plane(nc.sync, 0, quad)
+        load_x(1)
+        load_x(2)
+        load_x(3)
+        load_x(4)
+        nc.gpsimd.dma_start(out=bias_rows[0:P:32, :].rearrange("p (g i) -> p g i", g=G), in_=b.rearrange("g (k i) o -> k g (i o)", i=32))
+        load_words(nc.gpsimd, 1)
+        load_plane(nc.gpsimd, 1, 0)
+        nc.scalar.activation(out=warm_out[:, 0:1], in_=warm_in[:, 0:1], func=SILU)
+        for quad in range(1, 4):
+            load_plane(nc.scalar, 1, quad)
+
+        for step in [["cv",0],["cs",0],["b",0],["l",5],["q",0],["mm",0],["cv",1],["cs",1],["l",6],["s",0,0],["s",0,1],["q",1],["mm",1],["cv",2],["cs",2],["s",1,0],["s",1,1],["m",0,0],["q",2],["m",0,1],["mm",2],["cv",3],["cs",3],["s",2,0],["s",2,1],["m",1,0],["q",3],["m",1,1],["mm",3],["cv",4],["cs",4],["s",3,0],["s",3,1],["m",2,0],["q",4],["m",2,1],["mm",4],["cv",5],["cs",5],["s",4,0],["s",4,1],["m",3,0],["q",5],["m",3,1],["mm",5],["cv",6],["cs",6],["s",5,0],["s",5,1],["m",4,0],["q",6],["m",4,1],["mm",6],["cv",7],["cs",7],["s",6,0],["s",6,1],["m",5,0],["q",7],["m",5,1],["mm",7],["s",7,0],["s",7,1],["m",6,0],["m",6,1],["m",7,0],["m",7,1]]:
+            kind, u = step[0], step[1]
+            if kind == "cv":
+                copy_v(u)
+            elif kind == "cg":
+                copy_g(u)
+            elif kind == "cs":
+                copy_s(u)
+            elif kind == "q":
+                quantize(u)
+            elif kind == "mm":
+                multiply(u)
+            elif kind == "s":
+                silu(u, step[2])
+            elif kind == "m":
+                gate(u, step[2])
+            elif kind == "b":
+                nc.vector.transpose(out=bias_cols[:], in_=bias_rows[:])
+            elif kind == "l":
+                load_x(u)

@@ -18,12 +18,13 @@ ADD = mybir.AluOpType.add
 
 P = 128
 ROWS = 64
-UNIT = 256
-WIN = 512
-UNITS = 8
-V_COLS = [256,160,144,144,144,144,144,160]
+PIECE = 256
+STEP = 512
+PIECES = 8
+STEPS = 4
+V_COLS = [256,176,0,256,80,208,0,160]
 G_COLS = [0,0,0,0,0,0,0,0]
-LOADS = [[0,1],[1,1],[2,1],[3,1],[4,2],[6,1],[7,1]]
+RAW_BUFS = 5
 
 
 def tile_rows_gglu_silu_bias_kernel(tc, x, w_words, w_scales, u_words, u_scales, b, out):
@@ -40,24 +41,17 @@ def tile_rows_gglu_silu_bias_kernel(tc, x, w_words, w_scales, u_words, u_scales,
         bias_cols = keep.tile([P, P], F32, name="bias_cols", align_bytes=64)
         warm_in = keep.tile([P, 8], F32, name="warm_in")
         warm_out = keep.tile([P, 8], F32, name="warm_out")
-        codes = keep.tile([P, UNIT * (UNITS + 1)], U32, name="codes", align_bytes=64)
-        scales = keep.tile([P, UNIT * (UNITS + 1)], U8, name="scales", align_bytes=64)
-        raw = [keep.tile([P, 4, UNIT], F32, name="raw%d" % u, align_bytes=64) for u in range(2)]
-        raw_rest = keep.tile([P, 4, 4 * UNIT], F32, name="raw_rest", align_bytes=64)
-        grouped = [keep.tile([P, UNIT, 4], BF16, name="grouped%d" % u, align_bytes=64) for u in range(8)]
-        act = [keep.tile([P, 2, UNIT], F32, name="act%d" % u, align_bytes=64) for u in range(UNITS)]
-        y = [keep.tile([P, 2, N], F32, name="y%d" % q, align_bytes=64) for q in range(2)]
-        acc = [[[psum.tile([P, WIN], F32, name="acc%d%d%d" % (s, t, c)) for c in range(2)] for t in range(2)] for s in range(2)]
+        codes = keep.tile([P, PIECE * PIECES], U32, name="codes", align_bytes=64)
+        scales = keep.tile([P, PIECE * PIECES], U8, name="scales", align_bytes=64)
+        raw = [keep.tile([P, 4, PIECE], F32, name="raw%d" % u, align_bytes=64) for u in range(RAW_BUFS)]
+        grouped = [keep.tile([P, PIECE, 4], BF16, name="grouped%d" % u, align_bytes=64) for u in range(PIECES)]
+        act = [keep.tile([P, 2, STEP], F32, name="act%d" % s, align_bytes=64) for s in range(STEPS)]
+        y = [keep.tile([P, 2, STEP], F32, name="y%d" % s, align_bytes=64) for s in range(STEPS)]
+        acc = [[[psum.tile([P, STEP], F32, name="acc%d%d%d" % (s, t, c)) for c in range(2)] for t in range(2)] for s in range(2)]
 
-        def raw_of(u0, count):
-            if u0 < 2 or u0 >= 6:
-                return raw[u0 % 2][:, :, :]
-            return raw_rest[:, :, (u0 - 2) * UNIT : (u0 - 2 + count) * UNIT]
-
-        def load_x(i):
-            u0, count = LOADS[i]
-            n0 = (u0 % 4) * UNIT
-            nc.sync.dma_start(out=raw_of(u0, count), in_=x_pairs[u0 // 4][:, :, n0 : n0 + count * UNIT])
+        def load_x(u):
+            n0 = (u % 4) * PIECE
+            nc.sync.dma_start(out=raw[u % RAW_BUFS][:], in_=x_pairs[u // 4][:, :, n0 : n0 + PIECE])
 
         def load_words(eng, t):
             src = (w_words, u_words)[t].bitcast(I32).rearrange("(q c) p n -> (c p) q n", c=2)
@@ -68,72 +62,63 @@ def tile_rows_gglu_silu_bias_kernel(tc, x, w_words, w_scales, u_words, u_scales,
             eng.dma_start(out=planes[t][32 * quad : 32 * quad + 4].bitcast(I32), in_=src[quad // 2, quad % 2])
 
         def interleave(u, lo, hi):
-            src = raw_of(u, 1)[:, :, lo:hi].rearrange("p t (c i) -> p c t i", i=4)
-            dst = grouped[u % 8][:, lo:hi, :].rearrange("p (c i) t -> p c t i", i=4)
+            src = raw[u % RAW_BUFS][:, :, lo:hi].rearrange("p t (c i) -> p c t i", i=4)
+            dst = grouped[u][:, lo:hi, :].rearrange("p (c i) t -> p c t i", i=4)
             return src, dst
 
         def copy_v(u):
-            if V_COLS[u] > 0:
-                src, dst = interleave(u, 0, V_COLS[u])
-                nc.vector.tensor_copy(out=dst, in_=src)
+            src, dst = interleave(u, 0, V_COLS[u])
+            nc.vector.tensor_copy(out=dst, in_=src)
 
         def copy_g(u):
-            if G_COLS[u] > 0:
-                src, dst = interleave(u, V_COLS[u], V_COLS[u] + G_COLS[u])
-                nc.gpsimd.tensor_scalar(out=dst, in0=src, scalar1=1.0, scalar2=0.0, op0=MULT, op1=ADD)
+            src, dst = interleave(u, V_COLS[u], V_COLS[u] + G_COLS[u])
+            nc.gpsimd.tensor_scalar(out=dst, in0=src, scalar1=1.0, scalar2=0.0, op0=MULT, op1=ADD)
 
         def copy_s(u):
-            if V_COLS[u] + G_COLS[u] < UNIT:
-                src, dst = interleave(u, V_COLS[u] + G_COLS[u], UNIT)
-                nc.scalar.copy(out=dst, in_=src)
+            src, dst = interleave(u, V_COLS[u] + G_COLS[u], PIECE)
+            nc.scalar.copy(out=dst, in_=src)
 
         def quantize(u):
-            cols = slice((u + 1) * UNIT, (u + 2) * UNIT)
-            nc.vector.quantize_mx(out=codes[:, cols].bitcast(FP8X4), scales=scales[:, cols], in_=grouped[u % 8][:].rearrange("p n t -> p (n t)"))
+            cols = slice(u * PIECE, (u + 1) * PIECE)
+            nc.vector.quantize_mx(out=codes[:, cols].bitcast(FP8X4), scales=scales[:, cols], in_=grouped[u][:].rearrange("p n t -> p (n t)"))
 
-        def multiply(u):
-            win = slice(u * UNIT, u * UNIT + WIN)
-            for t in range(2):
-                for c in range(2):
-                    rows = slice(ROWS * c, ROWS * (c + 1))
-                    nc.tensor.matmul_mx(
-                        out=acc[u % 2][t][c][:],
-                        lhsT=words[t][rows, u // 4, :].bitcast(FP4X4),
-                        lhsT_scale=planes[t][rows, u // 4, :],
-                        rhs=codes[rows, win].bitcast(FP8X4),
-                        rhs_scale=scales[rows, win],
-                        start=True,
-                        stop=True,
-                    )
+        def multiply(s):
+            win = slice(s * STEP, (s + 1) * STEP)
+            for t, c in ((0, 0), (0, 1), (1, 0), (1, 1)):
+                rows = slice(ROWS * c, ROWS * (c + 1))
+                nc.tensor.matmul_mx(
+                    out=acc[s % 2][t][c][:],
+                    lhsT=words[t][rows, s // 2, :].bitcast(FP4X4),
+                    lhsT_scale=planes[t][rows, s // 2, :],
+                    rhs=codes[rows, win].bitcast(FP8X4),
+                    rhs_scale=scales[rows, win],
+                    start=True,
+                    stop=True,
+                )
 
-        def silu(u, c):
-            g = 2 * (u // 4) + c
-            nc.scalar.activation(out=act[u][:, c, :], in_=acc[u % 2][0][c][:, UNIT:WIN], func=SILU, bias=bias_cols[:, 32 * g : 32 * g + 1])
+        def silu(s, c):
+            g = 2 * (s // 2) + c
+            nc.scalar.activation(out=act[s][:, c, :], in_=acc[s % 2][0][c][:], func=SILU, bias=bias_cols[:, 32 * g : 32 * g + 1])
 
-        def gate(u, c):
-            n0 = (u % 4) * UNIT
-            nc.vector.tensor_tensor(out=y[u // 4][:, c, n0 : n0 + UNIT], in0=acc[u % 2][1][c][:, UNIT:WIN], in1=act[u][:, c, :], op=MULT)
-            q = u // 4
-            if u == UNITS - 1:
-                nc.sync.dma_start(out=out[2 * q + c, :, n0 : n0 + UNIT], in_=y[q][:, c, n0 : n0 + UNIT])
-            elif c == 1 and (u % 2 == 1 or u == UNITS - 2):
-                lo = n0 if u == UNITS - 2 else n0 - UNIT
-                nc.sync.dma_start(out=out[2 * q : 2 * q + 2, :, lo : n0 + UNIT].rearrange("c m n -> m c n"), in_=y[q][:, :, lo : n0 + UNIT])
+        def gate(s, c):
+            g = 2 * (s // 2) + c
+            n0 = (s % 2) * STEP
+            width = STEP // 2 if (s, c) == (STEPS - 1, 1) else STEP
+            for lo in range(0, STEP, width):
+                cols = slice(lo, lo + width)
+                nc.vector.tensor_tensor(out=y[s][:, c, cols], in0=acc[s % 2][1][c][:, cols], in1=act[s][:, c, cols], op=MULT)
+                nc.sync.dma_start(out=out[g, :, n0 + lo : n0 + lo + width], in_=y[s][:, c, cols])
 
         nc.vector.memset(planes[0][:].rearrange("p q m -> p (q m)").bitcast(I32), 0)
         nc.gpsimd.memset(bias_rows[:], 0.0)
         nc.vector.memset(warm_in[:], 0.0)
         nc.vector.memset(planes[1][:].rearrange("p q m -> p (q m)").bitcast(I32), 0)
-        nc.vector.memset(codes[:, 0:UNIT], 0)
-        nc.vector.memset(scales[:, 0:UNIT].bitcast(I32), 0)
         load_x(0)
         load_words(nc.sync, 0)
         for quad in range(4):
             load_plane(nc.sync, 0, quad)
-        load_x(1)
-        load_x(2)
-        load_x(3)
-        load_x(4)
+        for u in range(1, RAW_BUFS):
+            load_x(u)
         nc.gpsimd.dma_start(out=bias_rows[0:P:32, :].rearrange("p (g i) -> p g i", g=G), in_=b.rearrange("g (k i) o -> k g (i o)", i=32))
         load_words(nc.gpsimd, 1)
         load_plane(nc.gpsimd, 1, 0)
@@ -141,7 +126,7 @@ def tile_rows_gglu_silu_bias_kernel(tc, x, w_words, w_scales, u_words, u_scales,
         for quad in range(1, 4):
             load_plane(nc.scalar, 1, quad)
 
-        for step in [["cv",0],["cs",0],["b",0],["l",5],["q",0],["mm",0],["cv",1],["cs",1],["l",6],["s",0,0],["s",0,1],["q",1],["mm",1],["cv",2],["cs",2],["s",1,0],["s",1,1],["m",0,0],["q",2],["m",0,1],["mm",2],["cv",3],["cs",3],["s",2,0],["s",2,1],["m",1,0],["q",3],["m",1,1],["mm",3],["cv",4],["cs",4],["s",3,0],["s",3,1],["m",2,0],["q",4],["m",2,1],["mm",4],["cv",5],["cs",5],["s",4,0],["s",4,1],["m",3,0],["q",5],["m",3,1],["mm",5],["cv",6],["cs",6],["s",5,0],["s",5,1],["m",4,0],["q",6],["m",4,1],["mm",6],["cv",7],["cs",7],["s",6,0],["s",6,1],["m",5,0],["q",7],["m",5,1],["mm",7],["s",7,0],["s",7,1],["m",6,0],["m",6,1],["m",7,0],["m",7,1]]:
+        for step in [["cs",1],["cv",0],["l",5],["cs",2],["cv",1],["l",6],["l",7],["q",0],["q",1],["mm",0],["b",0],["s",0,0],["cv",3],["s",0,1],["q",2],["cs",4],["q",3],["mm",1],["cs",5],["cv",4],["s",1,0],["m",0,0],["cs",6],["cv",5],["cs",7],["q",4],["s",1,1],["q",5],["m",0,1],["mm",2],["s",2,0],["m",1,0],["s",2,1],["cv",7],["q",6],["q",7],["m",1,1],["mm",3],["s",3,0],["m",2,0],["s",3,1],["m",2,1],["m",3,0],["m",3,1]]:
             kind, u = step[0], step[1]
             if kind == "cv":
                 copy_v(u)

@@ -22,9 +22,9 @@ PIECE = 256
 STEP = 512
 PIECES = 8
 STEPS = 4
-V_COLS = [256,176,0,256,80,208,0,160]
+V_COLS = [208,160,256,224,0,160,176,144]
 G_COLS = [0,0,0,0,0,0,0,0]
-RAW_BUFS = 5
+RAW_BUFS = 8
 
 
 def tile_rows_gglu_silu_bias_kernel(tc, x, w_words, w_scales, u_words, u_scales, b, out):
@@ -113,20 +113,21 @@ def tile_rows_gglu_silu_bias_kernel(tc, x, w_words, w_scales, u_words, u_scales,
         nc.gpsimd.memset(bias_rows[:], 0.0)
         nc.vector.memset(warm_in[:], 0.0)
         nc.vector.memset(planes[1][:].rearrange("p q m -> p (q m)").bitcast(I32), 0)
-        load_x(0)
+        nc.scalar.activation(out=warm_out[:, 0:1], in_=warm_in[:, 0:1], func=SILU)
         load_words(nc.sync, 0)
+        load_x(0)
         for quad in range(4):
             load_plane(nc.sync, 0, quad)
-        for u in range(1, RAW_BUFS):
+        nc.sync.dma_start(out=bias_rows[0:P:32, :].rearrange("p (g i) -> p g i", g=G), in_=b.rearrange("g (k i) o -> k g (i o)", i=32))
+        load_x(1)
+        load_x(2)
+        load_words(nc.sync, 1)
+        for quad in range(4):
+            load_plane(nc.sync, 1, quad)
+        for u in range(3, PIECES):
             load_x(u)
-        nc.gpsimd.dma_start(out=bias_rows[0:P:32, :].rearrange("p (g i) -> p g i", g=G), in_=b.rearrange("g (k i) o -> k g (i o)", i=32))
-        load_words(nc.gpsimd, 1)
-        load_plane(nc.gpsimd, 1, 0)
-        nc.scalar.activation(out=warm_out[:, 0:1], in_=warm_in[:, 0:1], func=SILU)
-        for quad in range(1, 4):
-            load_plane(nc.scalar, 1, quad)
 
-        for step in [["cs",1],["cv",0],["l",5],["cs",2],["cv",1],["l",6],["l",7],["q",0],["q",1],["mm",0],["b",0],["s",0,0],["cv",3],["s",0,1],["q",2],["cs",4],["q",3],["mm",1],["cs",5],["cv",4],["s",1,0],["m",0,0],["cs",6],["cv",5],["cs",7],["q",4],["s",1,1],["q",5],["m",0,1],["mm",2],["s",2,0],["m",1,0],["s",2,1],["cv",7],["q",6],["q",7],["m",1,1],["mm",3],["s",3,0],["m",2,0],["s",3,1],["m",2,1],["m",3,0],["m",3,1]]:
+        for step in [["cs",0],["cv",0],["cs",1],["q",0],["cv",1],["b",0],["q",1],["mm",0],["s",0,0],["cv",2],["cs",3],["q",2],["s",0,1],["cv",3],["cs",4],["q",3],["mm",1],["cs",5],["m",0,0],["s",1,1],["m",0,1],["s",1,0],["cv",5],["cs",6],["q",4],["cs",7],["q",5],["mm",2],["s",2,1],["cv",6],["s",2,0],["m",1,1],["cv",7],["q",6],["q",7],["m",1,0],["mm",3],["s",3,0],["m",2,1],["s",3,1],["m",2,0],["m",3,0],["m",3,1]]:
             kind, u = step[0], step[1]
             if kind == "cv":
                 copy_v(u)

@@ -22,9 +22,9 @@ PIECE = 256
 STEP = 512
 PIECES = 8
 STEPS = 4
-V_COLS = [208,160,256,224,0,160,176,144]
+V_COLS = [256,112,256,96,256,48,256,48]
 G_COLS = [0,0,0,0,0,0,0,0]
-RAW_BUFS = 8
+LOADS = [[0,2],[2,2],[4,2],[6,2]]
 
 
 def tile_rows_gglu_silu_bias_kernel(tc, x, w_words, w_scales, u_words, u_scales, b, out):
@@ -43,15 +43,17 @@ def tile_rows_gglu_silu_bias_kernel(tc, x, w_words, w_scales, u_words, u_scales,
         warm_out = keep.tile([P, 8], F32, name="warm_out")
         codes = keep.tile([P, PIECE * PIECES], U32, name="codes", align_bytes=64)
         scales = keep.tile([P, PIECE * PIECES], U8, name="scales", align_bytes=64)
-        raw = [keep.tile([P, 4, PIECE], F32, name="raw%d" % u, align_bytes=64) for u in range(RAW_BUFS)]
+        raw = [keep.tile([P, 4, count * PIECE], F32, name="raw%d" % u0, align_bytes=64) for u0, count in LOADS]
+        raw_of = [raw[i][:, :, k * PIECE : (k + 1) * PIECE] for i in range(len(LOADS)) for k in range(LOADS[i][1])]
         grouped = [keep.tile([P, PIECE, 4], BF16, name="grouped%d" % u, align_bytes=64) for u in range(PIECES)]
         act = [keep.tile([P, 2, STEP], F32, name="act%d" % s, align_bytes=64) for s in range(STEPS)]
         y = [keep.tile([P, 2, STEP], F32, name="y%d" % s, align_bytes=64) for s in range(STEPS)]
         acc = [[[psum.tile([P, STEP], F32, name="acc%d%d%d" % (s, t, c)) for c in range(2)] for t in range(2)] for s in range(2)]
 
-        def load_x(u):
-            n0 = (u % 4) * PIECE
-            nc.sync.dma_start(out=raw[u % RAW_BUFS][:], in_=x_pairs[u // 4][:, :, n0 : n0 + PIECE])
+        def load_x(i):
+            u0, count = LOADS[i]
+            n0 = (u0 % 4) * PIECE
+            nc.sync.dma_start(out=raw[i][:], in_=x_pairs[u0 // 4][:, :, n0 : n0 + count * PIECE])
 
         def load_words(eng, t):
             src = (w_words, u_words)[t].bitcast(I32).rearrange("(q c) p n -> (c p) q n", c=2)
@@ -62,7 +64,7 @@ def tile_rows_gglu_silu_bias_kernel(tc, x, w_words, w_scales, u_words, u_scales,
             eng.dma_start(out=planes[t][32 * quad : 32 * quad + 4].bitcast(I32), in_=src[quad // 2, quad % 2])
 
         def interleave(u, lo, hi):
-            src = raw[u % RAW_BUFS][:, :, lo:hi].rearrange("p t (c i) -> p c t i", i=4)
+            src = raw_of[u][:, :, lo:hi].rearrange("p t (c i) -> p c t i", i=4)
             dst = grouped[u][:, lo:hi, :].rearrange("p (c i) t -> p c t i", i=4)
             return src, dst
 
@@ -120,14 +122,13 @@ def tile_rows_gglu_silu_bias_kernel(tc, x, w_words, w_scales, u_words, u_scales,
             load_plane(nc.sync, 0, quad)
         nc.sync.dma_start(out=bias_rows[0:P:32, :].rearrange("p (g i) -> p g i", g=G), in_=b.rearrange("g (k i) o -> k g (i o)", i=32))
         load_x(1)
-        load_x(2)
         load_words(nc.sync, 1)
         for quad in range(4):
             load_plane(nc.sync, 1, quad)
-        for u in range(3, PIECES):
+        for u in range(2, len(LOADS)):
             load_x(u)
 
-        for step in [["cs",0],["cv",0],["cs",1],["q",0],["cv",1],["b",0],["q",1],["mm",0],["s",0,0],["cv",2],["cs",3],["q",2],["s",0,1],["cv",3],["cs",4],["q",3],["mm",1],["cs",5],["m",0,0],["s",1,1],["m",0,1],["s",1,0],["cv",5],["cs",6],["q",4],["cs",7],["q",5],["mm",2],["s",2,1],["cv",6],["s",2,0],["m",1,1],["cv",7],["q",6],["q",7],["m",1,0],["mm",3],["s",3,0],["m",2,1],["s",3,1],["m",2,0],["m",3,0],["m",3,1]]:
+        for step in [["cs",1],["cv",0],["cs",3],["cv",1],["q",0],["q",1],["mm",0],["b",0],["s",0,0],["cv",2],["s",0,1],["cv",3],["cs",5],["q",2],["q",3],["mm",1],["s",1,0],["m",0,0],["s",1,1],["m",0,1],["cs",7],["cv",4],["cv",5],["q",4],["q",5],["mm",2],["s",2,0],["m",1,0],["s",2,1],["cv",6],["cv",7],["q",6],["q",7],["m",1,1],["mm",3],["s",3,0],["m",2,0],["s",3,1],["m",2,1],["m",3,0],["m",3,1]]:
             kind, u = step[0], step[1]
             if kind == "cv":
                 copy_v(u)

from contextlib import ExitStack

import concourse.mybir as mybir

G, D, M, N = 4, 256, 128, 1024
FLOPS = 2 * 2 * G * D * M * N

F32 = mybir.dt.float32
BF16 = mybir.dt.bfloat16
I32 = mybir.dt.int32
U32 = mybir.dt.uint32
U8 = mybir.dt.uint8
FP8X4 = mybir.dt.float8_e4m3fn_x4
FP4X4 = mybir.dt.float4_e2m1fn_x4
SILU = mybir.ActivationFunctionType.Silu
MULT = mybir.AluOpType.mult
ADD = mybir.AluOpType.add

P = 128
ROWS = 64
PIECE = 256
STEP = 512
PIECES = 8
STEPS = 4
V_COLS = [256,112,256,96,256,48,256,48]
G_COLS = [0,0,0,0,0,0,0,0]
LOADS = [[0,2],[2,2],[4,2],[6,2]]


def tile_rows_gglu_silu_bias_kernel(tc, x, w_words, w_scales, u_words, u_scales, b, out):
    nc = tc.nc
    with ExitStack() as ctx:
        keep = ctx.enter_context(tc.tile_pool(name="keep", bufs=1))
        psum = ctx.enter_context(tc.psum_pool(name="psum", bufs=1))
        ctx.enter_context(tc.manual_schedule())

        x_pairs = x.rearrange("(q c) (p j) n -> q (c p) j n", c=2, j=4)
        words = [keep.tile([P, 2, 2 * M], U8, name="words%d" % t, align_bytes=64) for t in range(2)]
        planes = [keep.tile([P, 2, M], U8, name="planes%d" % t, align_bytes=64) for t in range(2)]
        bias_rows = keep.tile([P, P], F32, name="bias_rows", align_bytes=64)
        bias_cols = keep.tile([P, P], F32, name="bias_cols", align_bytes=64)
        warm_in = keep.tile([P, 8], F32, name="warm_in")
        warm_out = keep.tile([P, 8], F32, name="warm_out")
        codes = keep.tile([P, PIECE * PIECES], U32, name="codes", align_bytes=64)
        scales = keep.tile([P, PIECE * PIECES], U8, name="scales", align_bytes=64)
        raw = [keep.tile([P, 4, count * PIECE], F32, name="raw%d" % u0, align_bytes=64) for u0, count in LOADS]
        raw_of = [raw[i][:, :, k * PIECE : (k + 1) * PIECE] for i in range(len(LOADS)) for k in range(LOADS[i][1])]
        grouped = [keep.tile([P, PIECE, 4], BF16, name="grouped%d" % u, align_bytes=64) for u in range(PIECES)]
        act = [keep.tile([P, 2, STEP], F32, name="act%d" % s, align_bytes=64) for s in range(STEPS)]
        y = [keep.tile([P, 2, STEP], F32, name="y%d" % s, align_bytes=64) for s in range(STEPS)]
        acc = [[[psum.tile([P, STEP], F32, name="acc%d%d%d" % (s, t, c)) for c in range(2)] for t in range(2)] for s in range(2)]

        def load_x(i):
            u0, count = LOADS[i]
            n0 = (u0 % 4) * PIECE
            nc.sync.dma_start(out=raw[i][:], in_=x_pairs[u0 // 4][:, :, n0 : n0 + count * PIECE])

        def load_words(eng, t):
            src = (w_words, u_words)[t].bitcast(I32).rearrange("(q c) p n -> (c p) q n", c=2)
            eng.dma_start(out=words[t][:].bitcast(I32), in_=src)

        def load_plane(eng, t, quad):
            src = (w_scales, u_scales)[t].bitcast(I32).rearrange("(q c) (h r) m -> c h r q m", c=2, h=2)
            eng.dma_start(out=planes[t][32 * quad : 32 * quad + 4].bitcast(I32), in_=src[quad // 2, quad % 2])

        def interleave(u, lo, hi):
            src = raw_of[u][:, :, lo:hi].rearrange("p t (c i) -> p c t i", i=4)
            dst = grouped[u][:, lo:hi, :].rearrange("p (c i) t -> p c t i", i=4)
            return src, dst

        def copy_v(u):
            src, dst = interleave(u, 0, V_COLS[u])
            nc.vector.tensor_copy(out=dst, in_=src)

        def copy_g(u):
            src, dst = interleave(u, V_COLS[u], V_COLS[u] + G_COLS[u])
            nc.gpsimd.tensor_scalar(out=dst, in0=src, scalar1=1.0, scalar2=0.0, op0=MULT, op1=ADD)

        def copy_s(u):
            src, dst = interleave(u, V_COLS[u] + G_COLS[u], PIECE)
            nc.scalar.copy(out=dst, in_=src)

        def quantize(u):
            cols = slice(u * PIECE, (u + 1) * PIECE)
            nc.vector.quantize_mx(out=codes[:, cols].bitcast(FP8X4), scales=scales[:, cols], in_=grouped[u][:].rearrange("p n t -> p (n t)"))

        def multiply(s):
            win = slice(s * STEP, (s + 1) * STEP)
            for t, c in ((0, 0), (0, 1), (1, 0), (1, 1)):
                rows = slice(ROWS * c, ROWS * (c + 1))
                nc.tensor.matmul_mx(
                    out=acc[s % 2][t][c][:],
                    lhsT=words[t][rows, s // 2, :].bitcast(FP4X4),
                    lhsT_scale=planes[t][rows, s // 2, :],
                    rhs=codes[rows, win].bitcast(FP8X4),
                    rhs_scale=scales[rows, win],
                    start=True,
                    stop=True,
                )

        def silu(s, c):
            g = 2 * (s // 2) + c
            nc.scalar.activation(out=act[s][:, c, :], in_=acc[s % 2][0][c][:], func=SILU, bias=bias_cols[:, 32 * g : 32 * g + 1])

        def gate(s, c):
            g = 2 * (s // 2) + c
            n0 = (s % 2) * STEP
            width = STEP // 2 if (s, c) == (STEPS - 1, 1) else STEP
            for lo in range(0, STEP, width):
                cols = slice(lo, lo + width)
                nc.vector.tensor_tensor(out=y[s][:, c, cols], in0=acc[s % 2][1][c][:, cols], in1=act[s][:, c, cols], op=MULT)
                nc.sync.dma_start(out=out[g, :, n0 + lo : n0 + lo + width], in_=y[s][:, c, cols])

        nc.vector.memset(planes[0][:].rearrange("p q m -> p (q m)").bitcast(I32), 0)
        nc.gpsimd.memset(bias_rows[:], 0.0)
        nc.vector.memset(warm_in[:], 0.0)
        nc.vector.memset(planes[1][:].rearrange("p q m -> p (q m)").bitcast(I32), 0)
        nc.scalar.activation(out=warm_out[:, 0:1], in_=warm_in[:, 0:1], func=SILU)
        load_words(nc.sync, 0)
        load_x(0)
        for quad in range(4):
            load_plane(nc.sync, 0, quad)
        nc.sync.dma_start(out=bias_rows[0:P:32, :].rearrange("p (g i) -> p g i", g=G), in_=b.rearrange("g (k i) o -> k g (i o)", i=32))
        load_x(1)
        load_words(nc.sync, 1)
        for quad in range(4):
            load_plane(nc.sync, 1, quad)
        for u in range(2, len(LOADS)):
            load_x(u)

        for step in [["cs",1],["cv",0],["cs",3],["cv",1],["q",0],["q",1],["mm",0],["b",0],["s",0,0],["cv",2],["s",0,1],["cv",3],["cs",5],["q",2],["q",3],["mm",1],["s",1,0],["m",0,0],["s",1,1],["m",0,1],["cs",7],["cv",4],["cv",5],["q",4],["q",5],["mm",2],["s",2,0],["m",1,0],["s",2,1],["cv",6],["cv",7],["q",6],["q",7],["m",1,1],["mm",3],["s",3,0],["m",2,0],["s",3,1],["m",2,1],["m",3,0],["m",3,1]]:
            kind, u = step[0], step[1]
            if kind == "cv":
                copy_v(u)
            elif kind == "cg":
                copy_g(u)
            elif kind == "cs":
                copy_s(u)
            elif kind == "q":
                quantize(u)
            elif kind == "mm":
                multiply(u)
            elif kind == "s":
                silu(u, step[2])
            elif kind == "m":
                gate(u, step[2])
            elif kind == "b":
                nc.vector.transpose(out=bias_cols[:], in_=bias_rows[:])
            elif kind == "l":
                load_x(u)
